import numpy as np
import ml_dtypes


def mxq(x, axis, fmt="e4m3"):
    dtype, down = {"e4m3": (ml_dtypes.float8_e4m3fn, 7), "e5m2": (ml_dtypes.float8_e5m2, 14)}[fmt]
    v = np.moveaxis(np.asarray(x, np.float32).astype(ml_dtypes.bfloat16).astype(np.float64), axis, -1)
    blocks = v.reshape(v.shape[:-1] + (-1, 32))
    amax = np.abs(blocks).max(-1, keepdims=True)
    byte = np.maximum(np.where(amax > 0, np.frexp(amax)[1] - 1 + 127, 0) - down, 1)
    scale = np.exp2(byte - 127.0)
    codes = (blocks / scale).astype(np.float32).astype(dtype).astype(np.float64)
    return np.moveaxis((codes * scale).reshape(v.shape), -1, axis)


WIDE = False


def mx_kscale(k):
    if not WIDE:
        return np.ones(k)
    levels = np.array([10, -10, 5, -5, 0])
    if k % 512:
        return np.exp2(np.random.permutation(np.resize(levels, k // 32))).repeat(32)
    a = np.empty((k // 512, 16))
    for p in range(k // 512):
        a[p, :8] = np.random.permutation(np.resize(levels, 8))
        for g in range(8):
            far = levels[np.abs(levels - a[p, g]) >= 10]
            a[p, g + 8] = far[np.random.randint(len(far))]
    return np.exp2(a.ravel()).repeat(32)


def f64(x):
    return np.asarray(x).astype(np.float64)


def striped8(idx):
    return np.asarray(idx).reshape(8, -1, 16).transpose(0, 2, 1).reshape(128, -1).astype(np.uint16)


def unstriped8(offs):
    return offs.reshape(8, 16, -1).transpose(0, 2, 1).reshape(8, -1).astype(np.int64)


def pick8(x, idx, run):
    r = np.arange(len(x))
    return x[r[:, None], idx[r % (8 * run) // run]]


E2M1 = np.array([0.0, 0.5, 1.0, 1.5, 2.0, 3.0, 4.0, 6.0, -0.0, -0.5, -1.0, -1.5, -2.0, -3.0, -4.0, -6.0])


def pack_weight(w, fmt):
    k, n = w.shape
    w = f64(np.asarray(w, np.float32).astype(ml_dtypes.bfloat16)).reshape(k // 32, 32, n)
    amax = np.abs(w).max(1)
    if fmt == "e4m3":
        byte = np.frexp(amax)[1] - 1 + 127 - 7
    else:
        mant, ex = np.frexp(amax / 6.0)
        byte = np.where(mant > 0.5, ex, ex - 1) + 127
    byte = np.clip(np.where(amax > 0, byte, 1), 1, 254)
    scaled = (w * np.exp2(127.0 - byte)[:, None, :]).reshape(k, n).astype(np.float32)
    by_word = np.ascontiguousarray(scaled.reshape(k // 512, 128, 4, n).transpose(0, 1, 3, 2))
    if fmt == "e4m3":
        words = by_word.astype(ml_dtypes.float8_e4m3fn).view(np.uint8)
    else:
        c = by_word.astype(ml_dtypes.float4_e2m1fn).view(np.uint8) & 0xF
        words = (c[..., 0::2] | (c[..., 1::2] << 4)).reshape(k // 512, 128, 2 * n)
    return np.ascontiguousarray(words), np.ascontiguousarray(byte.astype(np.uint8).reshape(k // 512, 16, n))


def unpack_weight(words, scales, fmt):
    g, _, n = scales.shape
    words = np.ascontiguousarray(words).reshape(g, 128, n, -1)
    if fmt == "e4m3":
        vals = words.view(ml_dtypes.float8_e4m3fn).astype(np.float64)
    else:
        nib = np.empty((g, 128, n, 4), np.uint8)
        nib[..., 0::2] = words & 0xF
        nib[..., 1::2] = words >> 4
        vals = E2M1[nib]
    vals = vals * np.repeat(np.exp2(scales.astype(np.float64) - 127.0), 8, axis=1)[..., None]
    return vals.transpose(0, 1, 3, 2).reshape(g * 512, n)


D, T, U, X, I, Q = 512, 1024, 1024, 1024, 512, 128


def setup_inputs():
    n = np.random.standard_normal
    idx = np.stack([np.random.permutation(T)[:I] for _ in range(8)])
    idx2 = np.stack([np.random.permutation(U)[:I] for _ in range(8)])
    idx3 = np.stack([np.random.permutation(X)[:I] for _ in range(8)])
    idx4 = np.stack([np.random.permutation(U)[:I] for _ in range(8)])
    idx5 = np.stack([np.random.permutation(X)[:I] for _ in range(8)])
    fd = mx_kscale(D)
    keysp = pack_weight(n((D, T)) / fd[:, None], "e4m3")
    notesp = pack_weight(n((D, U)) / fd[:, None], "e2m1")
    usersp = pack_weight(n((D, X)) / fd[:, None], "e4m3")
    return {
        "query": (n((D, Q)) * 1.0 / np.sqrt(D) * fd[:, None]).astype(np.float32),
        "keys_words": keysp[0],
        "keys_scales": keysp[1],
        "notes_words": notesp[0],
        "notes_scales": notesp[1],
        "users_words": usersp[0],
        "users_scales": usersp[1],
        "offs": striped8(idx),
        "offs2": striped8(idx2),
        "offs3": striped8(idx3),
        "offs4": striped8(idx4),
        "offs5": striped8(idx5),
    }


def reference(query, keys_words, keys_scales, notes_words, notes_scales, users_words, users_scales, offs, offs2, offs3, offs4, offs5):
    idx = unstriped8(offs)
    idx2 = unstriped8(offs2)
    idx3 = unstriped8(offs3)
    idx4 = unstriped8(offs4)
    idx5 = unstriped8(offs5)
    keysu = unpack_weight(keys_words, keys_scales, "e4m3")
    notesu = unpack_weight(notes_words, notes_scales, "e2m1")
    usersu = unpack_weight(users_words, users_scales, "e4m3")
    queryq = mxq(f64(query), 0, "e4m3")
    a = queryq.T @ keysu
    b = queryq.T @ notesu
    c0 = queryq.T @ usersu
    f1 = np.zeros((Q, U))
    f1[np.arange(Q)[:, None], idx2[np.arange(Q) % 128 // 16]] = pick8(a, idx, 16)
    f2 = np.zeros((Q, X))
    f2[np.arange(Q)[:, None], idx3[np.arange(Q) % 128 // 16]] = pick8(a, idx, 16)
    bb = b + f1
    cc = c0 - f2
    y = np.maximum(pick8(bb, idx4, 16), pick8(cc, idx5, 16))
    return y

@@ -1,0 +1,137 @@
+from contextlib import ExitStack
+
+import concourse.mybir as mybir
+
+F32 = mybir.dt.float32
+BF16 = mybir.dt.bfloat16
+I32 = mybir.dt.int32
+U32 = mybir.dt.uint32
+U16 = mybir.dt.uint16
+U8 = mybir.dt.uint8
+FP8X4 = mybir.dt.float8_e4m3fn_x4
+FP4X4 = mybir.dt.float4_e2m1fn_x4
+COPY = mybir.ActivationFunctionType.Copy
+ADD = mybir.AluOpType.add
+SUB = mybir.AluOpType.subtract
+MAX = mybir.AluOpType.max
+
+P = 128
+PACK = 4
+POOL = 1024
+SLOTS = 512
+BANK = 512
+HALF = SLOTS // 2
+LIST_COLS = SLOTS // 16
+FLOPS = 3 * 2 * 512 * 128 * 1024
+
+
+def tile_attend_sentboth_three_kernel(
+    tc, query, keys_words, keys_scales, notes_words, notes_scales, users_words, users_scales,
+    offs, offs2, offs3, offs4, offs5, out,
+):
+    nc = tc.nc
+    with ExitStack() as ctx:
+        keep = ctx.enter_context(tc.tile_pool(name="keep", bufs=1))
+        psum = ctx.enter_context(tc.psum_pool(name="psum", bufs=1))
+
+        def scale_tile(name):
+            t = keep.tile([P, POOL], U8, name=name, align_bytes=64)
+            nc.vector.memset(t[:].bitcast(U32), 0)
+            return t
+
+        def load_scales(t, dram):
+            for q in range(4):
+                nc.sync.dma_start(out=t[32 * q : 32 * q + 4, :].bitcast(I32), in_=dram[0][4 * q : 4 * q + 4, :].bitcast(I32))
+
+        def load_list(name, dram):
+            t = keep.tile([P, LIST_COLS], U16, name=name)
+            nc.sync.dma_start(t[:], dram)
+            return t
+
+        def load_words8(name, dram, h):
+            t = keep.tile([P, BANK], U32, name=name, align_bytes=64)
+            src = dram[0].rearrange("p n t -> p (n t)")[:, h * BANK * PACK : (h + 1) * BANK * PACK]
+            nc.sync.dma_start(out=t[:].bitcast(I32), in_=src.bitcast(I32))
+            return t
+
+        keys_sc = scale_tile("keys_sc")
+        notes_sc = scale_tile("notes_sc")
+        users_sc = scale_tile("users_sc")
+        f1 = keep.tile([P, POOL], F32, name="f1")
+        f2 = keep.tile([P, POOL], F32, name="f2")
+        nc.vector.memset(f1[:], 0.0)
+        nc.vector.memset(f2[:], 0.0)
+
+        q_raw = keep.tile([P, PACK, P], F32, name="q_raw")
+        nc.sync.dma_start(out=q_raw[:], in_=query.rearrange("(p j) w -> p j w", j=PACK))
+        keys_w = [load_words8("keys_w0", keys_words, 0)]
+        load_scales(keys_sc, keys_scales)
+        keys_w.append(load_words8("keys_w1", keys_words, 1))
+        l1 = load_list("l1", offs)
+        l2 = load_list("l2", offs2)
+        notes_w = keep.tile([P, 2 * POOL], U8, name="notes_w", align_bytes=64)
+        nc.sync.dma_start(out=notes_w[:].bitcast(I32), in_=notes_words[0].bitcast(I32))
+        load_scales(notes_sc, notes_scales)
+        l3 = load_list("l3", offs3)
+        l4 = load_list("l4", offs4)
+        users_w = [load_words8("users_w%d" % h, users_words, h) for h in range(2)]
+        load_scales(users_sc, users_scales)
+        l5 = load_list("l5", offs5)
+
+        q_bf = keep.tile([P, P, PACK], BF16, name="q_bf", align_bytes=64)
+        nc.vector.tensor_copy(
+            out=q_bf[:].rearrange("p (c i) t -> p c t i", i=4),
+            in_=q_raw[:].rearrange("p t (c i) -> p c t i", i=4),
+        )
+        q_codes = keep.tile([P, P], U32, name="q_codes", align_bytes=64)
+        q_sc = keep.tile([P, P], U8, name="q_sc", align_bytes=64)
+        nc.vector.quantize_mx(out=q_codes[:].bitcast(FP8X4), scales=q_sc[:], in_=q_bf[:].rearrange("p w j -> p (w j)"))
+
+        def scores(name, rhs, rhs_scale):
+            bank = psum.tile([P, BANK], F32, name=name)
+            nc.tensor.matmul_mx(
+                out=bank[:], lhsT=q_codes[:].bitcast(FP8X4), lhsT_scale=q_sc[:],
+                rhs=rhs, rhs_scale=rhs_scale, start=True, stop=True,
+            )
+            return bank
+
+        cols = [slice(h * BANK, (h + 1) * BANK) for h in range(2)]
+        a_ps = [scores("a_ps%d" % h, keys_w[h][:].bitcast(FP8X4), keys_sc[:, cols[h]]) for h in range(2)]
+        b_ps = [
+            scores("b_ps%d" % h, notes_w[:, 2 * BANK * h : 2 * BANK * (h + 1)].bitcast(FP4X4), notes_sc[:, cols[h]])
+            for h in range(2)
+        ]
+        c_ps = [scores("c_ps%d" % h, users_w[h][:].bitcast(FP8X4), users_sc[:, cols[h]]) for h in range(2)]
+
+        lo, hi = slice(0, HALF), slice(HALF, SLOTS)
+        llo, lhi = slice(0, LIST_COLS // 2), slice(LIST_COLS // 2, LIST_COLS)
+
+        a = keep.tile([P, POOL], F32, name="a")
+        nc.scalar.activation(a[:, cols[0]], a_ps[0][:], COPY)
+        nc.vector.tensor_copy(a[:, cols[1]], a_ps[1][:])
+        ga = keep.tile([P, SLOTS], F32, name="ga")
+        nc.vector.tensor_copy(ga[:, lo], a[:].indirect(l1[:, llo]))
+        nc.scalar.activation(ga[:, hi], a[:].indirect(l1[:, lhi]), COPY)
+
+        bb = keep.tile([P, POOL], F32, name="bb")
+        cc = keep.tile([P, POOL], F32, name="cc")
+        nc.vector.tensor_copy(f1[:].indirect(l2[:]), ga[:])
+        nc.vector.tensor_copy(f2[:].indirect(l3[:, llo]), ga[:, lo])
+        for h in range(2):
+            nc.vector.tensor_tensor(bb[:, cols[h]], b_ps[h][:], f1[:, cols[h]], ADD)
+        nc.vector.tensor_copy(f2[:].indirect(l3[:, lhi]), ga[:, hi])
+        gb = keep.tile([P, SLOTS], F32, name="gb")
+        nc.scalar.activation(gb[:], bb[:].indirect(l4[:]), COPY)
+        for h in range(2):
+            nc.vector.tensor_tensor(cc[:, cols[h]], c_ps[h][:], f2[:, cols[h]], SUB)
+
+        gc_lo = keep.tile([P, HALF], F32, name="gc_lo")
+        gc_hi = keep.tile([P, HALF], F32, name="gc_hi")
+        nc.vector.tensor_copy(gc_lo[:], cc[:].indirect(l5[:, llo]))
+        nc.scalar.activation(gc_hi[:], cc[:].indirect(l5[:, lhi]), COPY)
+        y_lo = keep.tile([P, HALF], F32, name="y_lo")
+        y_hi = keep.tile([P, HALF], F32, name="y_hi")
+        nc.vector.tensor_tensor(y_lo[:], gb[:, lo], gc_lo[:], MAX)
+        nc.sync.dma_start(out=out[:, lo], in_=y_lo[:])
+        nc.vector.tensor_tensor(y_hi[:], gb[:, hi], gc_hi[:], MAX)
+        nc.scalar.dma_start(out=out[:, hi], in_=y_hi[:])

@@ -80,15 +80,20 @@ def tile_attend_sentboth_three_kernel(
 
         q_bf = keep.tile([P, P, PACK], BF16, name="q_bf", align_bytes=64)
         nc.vector.tensor_copy(
-            out=q_bf[:].rearrange("p (c i) t -> p c t i", i=4),
-            in_=q_raw[:].rearrange("p t (c i) -> p c t i", i=4),
+            out=q_bf[:, 0:64, :].rearrange("p (c i) t -> p c t i", i=4),
+            in_=q_raw[:, :, 0:64].rearrange("p t (c i) -> p c t i", i=4),
+        )
+        nc.scalar.activation(
+            q_bf[:, 64:128, :].rearrange("p (c i) t -> p c t i", i=4),
+            q_raw[:, :, 64:128].rearrange("p t (c i) -> p c t i", i=4),
+            COPY,
         )
         q_codes = keep.tile([P, P], U32, name="q_codes", align_bytes=64)
         q_sc = keep.tile([P, P], U8, name="q_sc", align_bytes=64)
         nc.vector.quantize_mx(out=q_codes[:].bitcast(FP8X4), scales=q_sc[:], in_=q_bf[:].rearrange("p w j -> p (w j)"))
 
-        def scores(name, rhs, rhs_scale):
-            bank = psum.tile([P, BANK], F32, name=name)
+        def scores(name, rhs, rhs_scale, n=BANK):
+            bank = psum.tile([P, n], F32, name=name)
             nc.tensor.matmul_mx(
                 out=bank[:], lhsT=q_codes[:].bitcast(FP8X4), lhsT_scale=q_sc[:],
                 rhs=rhs, rhs_scale=rhs_scale, start=True, stop=True,
@@ -96,7 +101,12 @@ def tile_attend_sentboth_three_kernel(
             return bank
 
         cols = [slice(h * BANK, (h + 1) * BANK) for h in range(2)]
-        a_ps = [scores("a_ps%d" % h, keys_w[h][:].bitcast(FP8X4), keys_sc[:, cols[h]]) for h in range(2)]
+        cuts = [0, 512, 768, 896, 1024]
+        a_ps = []
+        for j in range(4):
+            c0, c1 = cuts[j], cuts[j + 1]
+            h = c0 // BANK
+            a_ps.append(scores("a_ps%d" % j, keys_w[h][:, c0 - h * BANK : c1 - h * BANK].bitcast(FP8X4), keys_sc[:, c0:c1], c1 - c0))
         b_ps = [
             scores("b_ps%d" % h, notes_w[:, 2 * BANK * h : 2 * BANK * (h + 1)].bitcast(FP4X4), notes_sc[:, cols[h]])
             for h in range(2)
@@ -106,9 +116,12 @@ def tile_attend_sentboth_three_kernel(
         lo, hi = slice(0, HALF), slice(HALF, SLOTS)
         llo, lhi = slice(0, LIST_COLS // 2), slice(LIST_COLS // 2, LIST_COLS)
 
-        a = keep.tile([P, POOL], F32, name="a")
-        nc.scalar.activation(a[:, cols[0]], a_ps[0][:], COPY)
-        nc.vector.tensor_copy(a[:, cols[1]], a_ps[1][:])
+        a = keep.tile([P, POOL], F32, name="a", tag="scores")
+        for j in range(4):
+            if j % 2 == 0:
+                nc.scalar.activation(a[:, cuts[j] : cuts[j + 1]], a_ps[j][:], COPY)
+            else:
+                nc.vector.tensor_copy(a[:, cuts[j] : cuts[j + 1]], a_ps[j][:])
         ga = keep.tile([P, SLOTS], F32, name="ga")
         nc.vector.tensor_copy(ga[:, lo], a[:].indirect(l1[:, llo]))
         nc.scalar.activation(ga[:, hi], a[:].indirect(l1[:, lhi]), COPY)
@@ -116,14 +129,19 @@ def tile_attend_sentboth_three_kernel(
         bb = keep.tile([P, POOL], F32, name="bb")
         cc = keep.tile([P, POOL], F32, name="cc")
         nc.vector.tensor_copy(f1[:].indirect(l2[:]), ga[:])
-        nc.vector.tensor_copy(f2[:].indirect(l3[:, llo]), ga[:, lo])
+        nc.vector.tensor_copy(f2[:].indirect(l3[:]), ga[:])
+
+        share = 256
+        staged = keep.tile([P, POOL + share], F32, name="staged", tag="scores")
         for h in range(2):
-            nc.vector.tensor_tensor(bb[:, cols[h]], b_ps[h][:], f1[:, cols[h]], ADD)
-        nc.vector.tensor_copy(f2[:].indirect(l3[:, lhi]), ga[:, hi])
+            nc.scalar.activation(staged[:, cols[h]], b_ps[h][:], COPY)
+        nc.scalar.activation(staged[:, POOL:], c_ps[1][:, BANK - share :], COPY)
+        nc.gpsimd.tensor_tensor(bb[:], staged[:, :POOL], f1[:], ADD)
         gb = keep.tile([P, SLOTS], F32, name="gb")
         nc.scalar.activation(gb[:], bb[:].indirect(l4[:]), COPY)
-        for h in range(2):
-            nc.vector.tensor_tensor(cc[:, cols[h]], c_ps[h][:], f2[:, cols[h]], SUB)
+        nc.vector.tensor_tensor(cc[:, cols[0]], c_ps[0][:], f2[:, cols[0]], SUB)
+        nc.vector.tensor_tensor(cc[:, BANK : POOL - share], c_ps[1][:, : BANK - share], f2[:, BANK : POOL - share], SUB)
+        nc.gpsimd.tensor_tensor(cc[:, POOL - share :], staged[:, POOL:], f2[:, POOL - share :], SUB)
 
         gc_lo = keep.tile([P, HALF], F32, name="gc_lo")
         gc_hi = keep.tile([P, HALF], F32, name="gc_hi")

@@ -49,7 +49,7 @@ def tile_attend_sentboth_three_kernel(
             return t
 
         def load_words8(name, dram, h):
-            t = keep.tile([P, BANK], U32, name=name, align_bytes=64)
+            t = keep.tile([P, BANK], U32, name=name, tag=name, align_bytes=64)
             src = dram[0].rearrange("p n t -> p (n t)")[:, h * BANK * PACK : (h + 1) * BANK * PACK]
             nc.sync.dma_start(out=t[:].bitcast(I32), in_=src.bitcast(I32))
             return t
@@ -58,9 +58,7 @@ def tile_attend_sentboth_three_kernel(
         notes_sc = scale_tile("notes_sc")
         users_sc = scale_tile("users_sc")
         f1 = keep.tile([P, POOL], F32, name="f1")
-        f2 = keep.tile([P, POOL], F32, name="f2")
         nc.vector.memset(f1[:], 0.0)
-        nc.vector.memset(f2[:], 0.0)
 
         q_raw = keep.tile([P, PACK, P], F32, name="q_raw")
         nc.sync.dma_start(out=q_raw[:], in_=query.rearrange("(p j) w -> p j w", j=PACK))
@@ -78,7 +76,7 @@ def tile_attend_sentboth_three_kernel(
         load_scales(users_sc, users_scales)
         l5 = load_list("l5", offs5)
 
-        q_bf = keep.tile([P, P, PACK], BF16, name="q_bf", align_bytes=64)
+        q_bf = keep.tile([P, P, PACK], BF16, name="q_bf", tag="q_bf", align_bytes=64)
         nc.vector.tensor_copy(
             out=q_bf[:, 0:64, :].rearrange("p (c i) t -> p c t i", i=4),
             in_=q_raw[:, :, 0:64].rearrange("p t (c i) -> p c t i", i=4),
@@ -91,6 +89,9 @@ def tile_attend_sentboth_three_kernel(
         q_codes = keep.tile([P, P], U32, name="q_codes", align_bytes=64)
         q_sc = keep.tile([P, P], U8, name="q_sc", align_bytes=64)
         nc.vector.quantize_mx(out=q_codes[:].bitcast(FP8X4), scales=q_sc[:], in_=q_bf[:].rearrange("p w j -> p (w j)"))
+
+        f2 = keep.tile([P, POOL], F32, name="f2", tag="q_bf", align_bytes=64)
+        nc.gpsimd.memset(f2[:], 0.0)
 
         def scores(name, rhs, rhs_scale, n=BANK):
             bank = psum.tile([P, n], F32, name=name)
@@ -137,7 +138,7 @@ def tile_attend_sentboth_three_kernel(
             nc.scalar.activation(staged[:, cols[h]], b_ps[h][:], COPY)
         nc.scalar.activation(staged[:, POOL:], c_ps[1][:, BANK - share :], COPY)
         nc.gpsimd.tensor_tensor(bb[:], staged[:, :POOL], f1[:], ADD)
-        gb = keep.tile([P, SLOTS], F32, name="gb")
+        gb = keep.tile([P, SLOTS], F32, name="gb", tag="users_w1", align_bytes=64)
         nc.scalar.activation(gb[:], bb[:].indirect(l4[:]), COPY)
         nc.vector.tensor_tensor(cc[:, cols[0]], c_ps[0][:], f2[:, cols[0]], SUB)
         nc.vector.tensor_tensor(cc[:, BANK : POOL - share], c_ps[1][:, : BANK - share], f2[:, BANK : POOL - share], SUB)

from contextlib import ExitStack

import concourse.mybir as mybir

F32 = mybir.dt.float32
BF16 = mybir.dt.bfloat16
I32 = mybir.dt.int32
U32 = mybir.dt.uint32
U16 = mybir.dt.uint16
U8 = mybir.dt.uint8
FP8X4 = mybir.dt.float8_e4m3fn_x4
FP4X4 = mybir.dt.float4_e2m1fn_x4
COPY = mybir.ActivationFunctionType.Copy
ADD = mybir.AluOpType.add
SUB = mybir.AluOpType.subtract
MAX = mybir.AluOpType.max

P = 128
PACK = 4
POOL = 1024
SLOTS = 512
BANK = 512
HALF = SLOTS // 2
LIST_COLS = SLOTS // 16
FLOPS = 3 * 2 * 512 * 128 * 1024


def tile_attend_sentboth_three_kernel(
    tc, query, keys_words, keys_scales, notes_words, notes_scales, users_words, users_scales,
    offs, offs2, offs3, offs4, offs5, out,
):
    nc = tc.nc
    with ExitStack() as ctx:
        keep = ctx.enter_context(tc.tile_pool(name="keep", bufs=1))
        psum = ctx.enter_context(tc.psum_pool(name="psum", bufs=1))

        def scale_tile(name):
            t = keep.tile([P, POOL], U8, name=name, align_bytes=64)
            nc.vector.memset(t[:].bitcast(U32), 0)
            return t

        def load_scales(t, dram):
            for q in range(4):
                nc.sync.dma_start(out=t[32 * q : 32 * q + 4, :].bitcast(I32), in_=dram[0][4 * q : 4 * q + 4, :].bitcast(I32))

        def load_list(name, dram):
            t = keep.tile([P, LIST_COLS], U16, name=name)
            nc.sync.dma_start(t[:], dram)
            return t

        def load_words8(name, dram, h):
            t = keep.tile([P, BANK], U32, name=name, tag=name, align_bytes=64)
            src = dram[0].rearrange("p n t -> p (n t)")[:, h * BANK * PACK : (h + 1) * BANK * PACK]
            nc.sync.dma_start(out=t[:].bitcast(I32), in_=src.bitcast(I32))
            return t

        keys_sc = scale_tile("keys_sc")
        notes_sc = scale_tile("notes_sc")
        users_sc = scale_tile("users_sc")
        f1 = keep.tile([P, POOL], F32, name="f1")
        nc.vector.memset(f1[:], 0.0)

        q_raw = keep.tile([P, PACK, P], F32, name="q_raw")
        nc.sync.dma_start(out=q_raw[:], in_=query.rearrange("(p j) w -> p j w", j=PACK))
        keys_w = [load_words8("keys_w0", keys_words, 0)]
        load_scales(keys_sc, keys_scales)
        keys_w.append(load_words8("keys_w1", keys_words, 1))
        l1 = load_list("l1", offs)
        l2 = load_list("l2", offs2)
        notes_w = keep.tile([P, 2 * POOL], U8, name="notes_w", align_bytes=64)
        nc.sync.dma_start(out=notes_w[:].bitcast(I32), in_=notes_words[0].bitcast(I32))
        load_scales(notes_sc, notes_scales)
        l3 = load_list("l3", offs3)
        l4 = load_list("l4", offs4)
        users_w = [load_words8("users_w%d" % h, users_words, h) for h in range(2)]
        load_scales(users_sc, users_scales)
        l5 = load_list("l5", offs5)

        q_bf = keep.tile([P, P, PACK], BF16, name="q_bf", tag="q_bf", align_bytes=64)
        nc.vector.tensor_copy(
            out=q_bf[:, 0:64, :].rearrange("p (c i) t -> p c t i", i=4),
            in_=q_raw[:, :, 0:64].rearrange("p t (c i) -> p c t i", i=4),
        )
        nc.scalar.activation(
            q_bf[:, 64:128, :].rearrange("p (c i) t -> p c t i", i=4),
            q_raw[:, :, 64:128].rearrange("p t (c i) -> p c t i", i=4),
            COPY,
        )
        q_codes = keep.tile([P, P], U32, name="q_codes", align_bytes=64)
        q_sc = keep.tile([P, P], U8, name="q_sc", align_bytes=64)
        nc.vector.quantize_mx(out=q_codes[:].bitcast(FP8X4), scales=q_sc[:], in_=q_bf[:].rearrange("p w j -> p (w j)"))

        f2 = keep.tile([P, POOL], F32, name="f2", tag="q_bf", align_bytes=64)
        nc.gpsimd.memset(f2[:], 0.0)

        def scores(name, rhs, rhs_scale, n=BANK):
            bank = psum.tile([P, n], F32, name=name)
            nc.tensor.matmul_mx(
                out=bank[:], lhsT=q_codes[:].bitcast(FP8X4), lhsT_scale=q_sc[:],
                rhs=rhs, rhs_scale=rhs_scale, start=True, stop=True,
            )
            return bank

        cols = [slice(h * BANK, (h + 1) * BANK) for h in range(2)]
        cuts = [0, 512, 768, 896, 1024]
        a_ps = []
        for j in range(4):
            c0, c1 = cuts[j], cuts[j + 1]
            h = c0 // BANK
            a_ps.append(scores("a_ps%d" % j, keys_w[h][:, c0 - h * BANK : c1 - h * BANK].bitcast(FP8X4), keys_sc[:, c0:c1], c1 - c0))
        b_ps = [
            scores("b_ps%d" % h, notes_w[:, 2 * BANK * h : 2 * BANK * (h + 1)].bitcast(FP4X4), notes_sc[:, cols[h]])
            for h in range(2)
        ]
        c_ps = [scores("c_ps%d" % h, users_w[h][:].bitcast(FP8X4), users_sc[:, cols[h]]) for h in range(2)]

        lo, hi = slice(0, HALF), slice(HALF, SLOTS)
        llo, lhi = slice(0, LIST_COLS // 2), slice(LIST_COLS // 2, LIST_COLS)

        a = keep.tile([P, POOL], F32, name="a", tag="scores")
        for j in range(4):
            if j % 2 == 0:
                nc.scalar.activation(a[:, cuts[j] : cuts[j + 1]], a_ps[j][:], COPY)
            else:
                nc.vector.tensor_copy(a[:, cuts[j] : cuts[j + 1]], a_ps[j][:])
        ga = keep.tile([P, SLOTS], F32, name="ga")
        nc.vector.tensor_copy(ga[:, lo], a[:].indirect(l1[:, llo]))
        nc.scalar.activation(ga[:, hi], a[:].indirect(l1[:, lhi]), COPY)

        bb = keep.tile([P, POOL], F32, name="bb")
        cc = keep.tile([P, POOL], F32, name="cc")
        nc.vector.tensor_copy(f1[:].indirect(l2[:]), ga[:])
        nc.vector.tensor_copy(f2[:].indirect(l3[:]), ga[:])

        share = 256
        staged = keep.tile([P, POOL + share], F32, name="staged", tag="scores")
        for h in range(2):
            nc.scalar.activation(staged[:, cols[h]], b_ps[h][:], COPY)
        nc.scalar.activation(staged[:, POOL:], c_ps[1][:, BANK - share :], COPY)
        nc.gpsimd.tensor_tensor(bb[:], staged[:, :POOL], f1[:], ADD)
        gb = keep.tile([P, SLOTS], F32, name="gb", tag="users_w1", align_bytes=64)
        nc.scalar.activation(gb[:], bb[:].indirect(l4[:]), COPY)
        nc.vector.tensor_tensor(cc[:, cols[0]], c_ps[0][:], f2[:, cols[0]], SUB)
        nc.vector.tensor_tensor(cc[:, BANK : POOL - share], c_ps[1][:, : BANK - share], f2[:, BANK : POOL - share], SUB)
        nc.gpsimd.tensor_tensor(cc[:, POOL - share :], staged[:, POOL:], f2[:, POOL - share :], SUB)

        gc_lo = keep.tile([P, HALF], F32, name="gc_lo")
        gc_hi = keep.tile([P, HALF], F32, name="gc_hi")
        nc.vector.tensor_copy(gc_lo[:], cc[:].indirect(l5[:, llo]))
        nc.scalar.activation(gc_hi[:], cc[:].indirect(l5[:, lhi]), COPY)
        y_lo = keep.tile([P, HALF], F32, name="y_lo")
        y_hi = keep.tile([P, HALF], F32, name="y_hi")
        nc.vector.tensor_tensor(y_lo[:], gb[:, lo], gc_lo[:], MAX)
        nc.sync.dma_start(out=out[:, lo], in_=y_lo[:])
        nc.vector.tensor_tensor(y_hi[:], gb[:, hi], gc_hi[:], MAX)
        nc.scalar.dma_start(out=out[:, hi], in_=y_hi[:])
